import numpy as np
import ml_dtypes


def mxq(x, axis, fmt="e4m3"):
    dtype, down = {"e4m3": (ml_dtypes.float8_e4m3fn, 7), "e5m2": (ml_dtypes.float8_e5m2, 14)}[fmt]
    v = np.moveaxis(np.asarray(x, np.float32).astype(ml_dtypes.bfloat16).astype(np.float64), axis, -1)
    blocks = v.reshape(v.shape[:-1] + (-1, 32))
    amax = np.abs(blocks).max(-1, keepdims=True)
    byte = np.maximum(np.where(amax > 0, np.frexp(amax)[1] - 1 + 127, 0) - down, 1)
    scale = np.exp2(byte - 127.0)
    codes = (blocks / scale).astype(np.float32).astype(dtype).astype(np.float64)
    return np.moveaxis((codes * scale).reshape(v.shape), -1, axis)


WIDE = False


def mx_kscale(k):
    if not WIDE:
        return np.ones(k)
    levels = np.array([10, -10, 5, -5, 0])
    if k % 512:
        return np.exp2(np.random.permutation(np.resize(levels, k // 32))).repeat(32)
    a = np.empty((k // 512, 16))
    for p in range(k // 512):
        a[p, :8] = np.random.permutation(np.resize(levels, 8))
        for g in range(8):
            far = levels[np.abs(levels - a[p, g]) >= 10]
            a[p, g + 8] = far[np.random.randint(len(far))]
    return np.exp2(a.ravel()).repeat(32)


def f64(x):
    return np.asarray(x).astype(np.float64)


def striped(idx):
    return np.tile(idx.reshape(-1, 16).T, (8, 1)).astype(np.uint16)


def unstriped(offs):
    return offs[:16].T.reshape(-1).astype(np.int64)


def striped8(idx):
    return np.concatenate([x.reshape(-1, 16).T for x in idx]).astype(np.uint16)


def runs(offs, k):
    lists = np.stack([offs[16 * r : 16 * r + 16].T.reshape(-1) for r in range(8)]).astype(np.int64)
    return lists[np.arange(k) % 512 // 64]


def pack_weight(w):
    k, n = w.shape
    w = f64(np.asarray(w, np.float32).astype(ml_dtypes.bfloat16)).reshape(k // 32, 32, n)
    amax = np.abs(w).max(1)
    byte = np.clip(np.where(amax > 0, np.frexp(amax)[1] - 1 + 127 - 7, 1), 1, 254)
    scaled = (w * np.exp2(127.0 - byte)[:, None, :]).reshape(k, n).astype(np.float32)
    words = np.ascontiguousarray(scaled.reshape(k // 512, 128, 4, n).transpose(0, 1, 3, 2)).astype(ml_dtypes.float8_e4m3fn).view(np.uint8)
    return words, np.ascontiguousarray(byte.astype(np.uint8).reshape(k // 512, 16, n))


def unpack_weight(words, scales):
    g, p, n, _ = words.shape
    vals = np.ascontiguousarray(words).view(ml_dtypes.float8_e4m3fn).astype(np.float64) * np.repeat(np.exp2(scales.astype(np.float64) - 127.0), 8, axis=1)[..., None]
    return vals.transpose(0, 1, 3, 2).reshape(g * 512, n)

def planes(y):
    n, m = y.shape
    v = y.astype(np.float32).astype(ml_dtypes.bfloat16).astype(np.float64).reshape(n // 32, 32, m)
    top = np.abs(v).max(1)
    byte = np.clip(np.where(top > 0, np.frexp(top)[1] - 1 + 127 - 7, 1), 1, 254)
    codes = (v * np.exp2(127.0 - byte)[:, None, :]).reshape(n, m).astype(np.float32).astype(ml_dtypes.float8_e4m3fn).view(np.uint8)
    words = codes.reshape(n // 512, 128, 4, m).transpose(0, 1, 3, 2)
    return np.ascontiguousarray(words), np.ascontiguousarray(byte.astype(np.uint8).reshape(n // 512, 16, m))


K, T, S, N, G, H, W = 512, 1024, 512, 512, 2048, 512, 384


def setup_inputs():
    n = np.random.standard_normal
    s = mx_kscale(K)[:, None]
    u = mx_kscale(S)
    packed_xT = pack_weight(n((K, T)) * s)
    packed_dT = pack_weight(n((K, G)) / s)
    packed_w1 = pack_weight(n((H, N)) / np.sqrt(2 * H) / u[:, None])
    packed_w2 = pack_weight(n((K, N)) / np.sqrt(2 * K) / s)
    return {
        "x_words": packed_xT[0],
        "x_scales": packed_xT[1],
        "d_words": packed_dT[0],
        "d_scales": packed_dT[1],
        "gn": (np.random.uniform(0.5, 1.5, (H, 1)) * u[:, None]).astype(np.float32),
        "w1_words": packed_w1[0],
        "w1_scales": packed_w1[1],
        "w2_words": packed_w2[0],
        "w2_scales": packed_w2[1],
        "offs": striped(np.random.permutation(T)[:S]),
        "k1": striped8(np.random.randint(0, G, (8, H))),
        "n1": striped(np.random.permutation(S)[:W]),
        "n2": striped(np.random.permutation(S)[:W]),
        "two": striped(np.random.permutation(T)[:S]),
        "n3": striped8(np.stack([np.random.permutation(S) for _ in range(8)])),
        "n4": striped8(np.stack([np.random.permutation(S) for _ in range(8)])),
    }


def reference(x_words, x_scales, d_words, d_scales, gn, w1_words, w1_scales, w2_words, w2_scales, offs, k1, n1, n2, two, n3, n4):
    d_k1 = unpack_weight(d_words, d_scales)[np.arange(K)[:, None], runs(k1, K)]
    xq = unpack_weight(x_words, x_scales)[:, unstriped(offs)]
    h = 0.0625 * (d_k1.T @ xq)
    pa = h[:, unstriped(n2)]
    old = h[:, unstriped(n1)]
    ra = np.minimum(pa, old) - (0.5 * pa)
    ds = h.copy()
    ds[:, unstriped(n1)] = ra
    z = f64(gn) * ds
    x_two = unpack_weight(x_words, x_scales)[:, unstriped(two)]
    h2 = unpack_weight(w1_words, w1_scales).T @ mxq(z, 0, "e4m3") + unpack_weight(w2_words, w2_scales).T @ x_two
    out_0 = (h2[np.arange(N)[:, None], runs(n3, N)]) / (np.abs(h2) + np.abs(h2[np.arange(N)[:, None], runs(n4, N)]) + 0.5)
    return (out_0,) + planes(out_0)

@@ -1,0 +1,208 @@
+from contextlib import ExitStack
+
+import concourse.mybir as mybir
+
+F32 = mybir.dt.float32
+BF16 = mybir.dt.bfloat16
+I32 = mybir.dt.int32
+U32 = mybir.dt.uint32
+U16 = mybir.dt.uint16
+U8 = mybir.dt.uint8
+FP8X4 = mybir.dt.float8_e4m3fn_x4
+ALU = mybir.AluOpType
+ACT = mybir.ActivationFunctionType
+
+P = 128
+PACK = 4
+S = 512
+W = 384
+T = 1024
+G = 2048
+FLOPS = 3 * 2 * 512 * 512 * 512
+CHUNKS = [(0, 256), (256, 512)]
+
+
+def tile_picked_pqmixkminnorm2_none_po_kernel(
+    tc, x_words, x_scales, d_words, d_scales, gn, w1_words, w1_scales, w2_words, w2_scales,
+    offs, k1, n1, n2, two, n3, n4, out_0, out_1, out_2,
+):
+    nc = tc.nc
+
+    def words_of(ap):
+        return ap[0].rearrange("p c r -> p (c r)").bitcast(I32)
+
+    with ExitStack() as ctx:
+        sb = ctx.enter_context(tc.tile_pool(name="sb", bufs=1))
+        ps = ctx.enter_context(tc.psum_pool(name="ps", bufs=1))
+
+        def new(name, shape, dtype, tag=None, bufs=1):
+            return sb.tile(shape, dtype, name=name, tag=tag or name, bufs=bufs, align_bytes=64)
+
+        def spread(rows, times):
+            rows = rows.bitcast(I32)
+            return rows.unsqueeze(1).broadcast_to([rows.shape[0], times, rows.shape[1]])
+
+        def load_list(name, ap):
+            t = new(name, list(ap.shape), U16)
+            nc.sync.dma_start(t[:], ap)
+            return t
+
+        d_sc = new("d_sc", [P, S], U8)
+        nc.vector.memset(d_sc[:].bitcast(I32), 0)
+        half = new("half", [P, 1], F32)
+        nc.vector.memset(half[:], 0.5)
+
+        k1_t = load_list("k1_t", k1)
+        ds_win = new("ds_win", [P, G], U8, "early_a")
+        nc.sync.dma_start(ds_win[:].bitcast(I32), spread(d_scales[0], 8))
+        dw_win = new("dw_win", [P, G], U32)
+        nc.sync.dma_start(dw_win[:].bitcast(I32), words_of(d_words))
+        offs_t = load_list("offs_t", offs)
+        two_t = load_list("two_t", two)
+        n2_t = load_list("n2_t", n2)
+        n1_t = load_list("n1_t", n1)
+        xw_win = new("xw_win", [P, T], U32)
+        nc.sync.dma_start(xw_win[:].bitcast(I32), words_of(x_words))
+        n4_t = load_list("n4_t", n4)
+        n3_t = load_list("n3_t", n3)
+        xs_win = new("xs_win", [P, T], U8)
+        for j in range(4):
+            nc.gpsimd.dma_start(xs_win[j:P:4, :].bitcast(I32), spread(x_scales[0, j:16:4, :], 8))
+        gn_t = new("gn_t", [P, PACK], F32)
+        nc.gpsimd.dma_start(gn_t[:], gn.rearrange("(p t) o -> p (t o)", t=PACK))
+
+        def deal(eng, dst, src):
+            eng.tensor_copy(dst.rearrange("p (t m) -> p m t", t=PACK), src.rearrange("p (m t) -> p m t", t=PACK))
+
+        ds_g = new("ds_g", [P, S], U8, "early_b")
+        nc.vector.tensor_copy(ds_g[:], ds_win[:].indirect(k1_t[:]))
+        ds_d = new("ds_d", [P, S], U8)
+        deal(nc.vector, ds_d[:], ds_g[:])
+        for j in range(4):
+            nc.scalar.dma_start(d_sc[j:P:32, :].bitcast(I32), ds_d[8 * j : P : 32, :].bitcast(I32))
+        w_raw = new("w_raw", [P, 2, S], U32, "early_a")
+        nc.sync.dma_start(w_raw[:, 0, :].bitcast(I32), words_of(w1_words))
+        nc.sync.dma_start(w_raw[:, 1, :].bitcast(I32), words_of(w2_words))
+        ws_raw = new("ws_raw", [P, S], U8, "early_b")
+        for i, sc in enumerate((w1_scales, w2_scales)):
+            for j in range(4):
+                nc.sync.dma_start(ws_raw[4 * i + j : P : 8, :].bitcast(I32), spread(sc[0, j:16:4, :], 4))
+        dw_g = new("dw_g", [P, S], U32)
+        nc.vector.tensor_copy(dw_g[:], dw_win[:].indirect(k1_t[:]))
+        xw_g = new("xw_g", [P, S], U32)
+        nc.vector.tensor_copy(xw_g[:], xw_win[:].indirect(offs_t[:]))
+        dw_d = new("dw_d", [P, S], U32)
+        deal(nc.vector, dw_d[:], dw_g[:])
+        xs_g = new("xs_g", [P, S], U8)
+        nc.vector.tensor_copy(xs_g[:], xs_win[:].indirect(offs_t[:]))
+
+        hp = [ps.tile([P, S], F32, name=f"hp{t}") for t in range(PACK)]
+        h2p = [ps.tile([P, S], F32, name=f"h2p{t}") for t in range(PACK)]
+        for t in range(PACK):
+            c = slice(P * t, P * (t + 1))
+            nc.tensor.matmul_mx(hp[t][:], lhsT=dw_d[:, c].bitcast(FP8X4), lhsT_scale=d_sc[:, c],
+                                rhs=xw_g[:].bitcast(FP8X4), rhs_scale=xs_g[:], start=True, stop=True)
+
+        x2w_g = new("x2w_g", [P, S], U32)
+        nc.vector.tensor_copy(x2w_g[:], xw_win[:].indirect(two_t[:]))
+        x2s_g = new("x2s_g", [P, S], U8)
+        nc.vector.tensor_copy(x2s_g[:], xs_win[:].indirect(two_t[:]))
+
+        z_pl = new("z_pl", [P, PACK, S], BF16)
+        h = [new(f"h{t}", [P, S], F32) for t in range(PACK)]
+        nhp = [new(f"nhp{t}", [P, W], F32, f"mid_n{t}") for t in range(PACK)]
+        a = [new(f"a{t}", [P, W], F32, f"mid_a{t}") for t in range(PACK)]
+        ra = [new(f"ra{t}", [P, W], F32) for t in range(PACK)]
+        for k in range(PACK + 2):
+            if k < PACK:
+                nc.scalar.activation(h[k][:], hp[k][:], ACT.Copy, scale=0.0625)
+            t = k - 1
+            if 0 <= t < PACK:
+                nc.scalar.activation(nhp[t][:], h[t][:].indirect(n2_t[:]), ACT.Copy, scale=-0.5)
+                nc.vector.tensor_tensor(a[t][:], h[t][:].indirect(n1_t[:]), nhp[t][:], ALU.add)
+            t = k - 2
+            if 0 <= t < PACK:
+                nc.vector.scalar_tensor_tensor(ra[t][:], nhp[t][:], -1.0, a[t][:], ALU.mult, ALU.min)
+        for t in range(2):
+            nc.scalar.activation(h[t][:].indirect(n1_t[:]), ra[t][:], ACT.Copy)
+        nc.vector.tensor_copy(h[2][:].indirect(n1_t[:, 0:8]), ra[2][:, 0:128])
+        nc.vector.tensor_copy(h[3][:].indirect(n1_t[:]), ra[3][:])
+        nc.scalar.activation(h[2][:].indirect(n1_t[:, 8:24]), ra[2][:, 128:W], ACT.Copy)
+        w_d = new("w_d", [P, 2, S], U32, "mid_n3")
+        ws_d = new("ws_d", [P, S], U8, "mid_a3")
+        for i in range(2):
+            deal(nc.vector, w_d[:, i, :], w_raw[:, i, :])
+        deal(nc.vector, ws_d[:], ws_raw[:])
+        for t in range(PACK):
+            c = slice(P * t, P * (t + 1))
+            nc.tensor.matmul_mx(h2p[t][:], lhsT=w_d[:, 1, c].bitcast(FP8X4), lhsT_scale=ws_d[4:P, c],
+                                rhs=x2w_g[:].bitcast(FP8X4), rhs_scale=x2s_g[:], start=True, stop=False)
+        for t in (0, 1, 3):
+            nc.vector.tensor_scalar(z_pl[:, t, :], h[t][:], gn_t[:, t : t + 1], None, ALU.mult)
+        nc.scalar.activation(z_pl[:, 2, :], h[2][:], ACT.Copy, scale=gn_t[:, 2:3])
+        z_il = new("z_il", [P, S, PACK], BF16)
+        nc.vector.tensor_copy(z_il[:].rearrange("p (c i) t -> p c t i", i=4), z_pl[:].rearrange("p t (c i) -> p c t i", i=4))
+        z_w = new("z_w", [P, S], U32)
+        z_s = new("z_s", [P, S], U8)
+        nc.vector.quantize_mx(z_w[:].bitcast(FP8X4), z_s[:], z_il[:].rearrange("p c t -> p (c t)"))
+        for t in range(PACK):
+            c = slice(P * t, P * (t + 1))
+            nc.tensor.matmul_mx(h2p[t][:], lhsT=w_d[:, 0, c].bitcast(FP8X4), lhsT_scale=ws_d[:, c],
+                                rhs=z_w[:].bitcast(FP8X4), rhs_scale=z_s[:], start=False, stop=True)
+
+        h2 = [new(f"h2_{t}", [P, S], F32) for t in range(PACK)]
+        ab = [new(f"ab{t}", [P, S], F32) for t in range(PACK)]
+        out_rows = out_0.rearrange("(p t) c -> p t c", t=PACK)
+        o_w = new("o_w", [P, S], U32)
+        o_s = new("o_s", [P, S], U8)
+        units = [(ci, t) for ci in range(len(CHUNKS)) for t in range(PACK)]
+        ys = [new(f"y{ci}", [P, PACK, c1 - c0], F32) for ci, (c0, c1) in enumerate(CHUNKS)]
+        dens, roots, recs = {}, {}, {}
+
+        def fetch(ci, t):
+            c0, c1 = CHUNKS[ci]
+            g4 = new(f"g4_{ci}_{t}", [P, c1 - c0], F32, "g4", 2)
+            nc.scalar.activation(g4[:], ab[t][:].indirect(n4_t[:, c0 // 16 : c1 // 16]), ACT.Copy)
+            dens[ci, t] = new(f"den{ci}_{t}", [P, c1 - c0], F32)
+            nc.vector.tensor_tensor(dens[ci, t][:], g4[:], ab[t][:, c0:c1], ALU.add)
+
+        def root(ci, t):
+            c0, c1 = CHUNKS[ci]
+            roots[ci, t] = new(f"r{ci}_{t}", [P, c1 - c0], F32)
+            nc.scalar.activation(roots[ci, t][:], dens[ci, t][:], ACT.Abs_reciprocal_sqrt, bias=half[:])
+
+        def finish(ci, t):
+            c0, c1 = CHUNKS[ci]
+            cols = slice(c0, c1)
+            n = c1 - c0
+            rec = new(f"rec{ci}_{t}", [P, n], F32)
+            nc.scalar.activation(rec[:], roots[ci, t][:], ACT.Square)
+            y = ys[ci]
+            nc.vector.tensor_tensor(y[:, t, :], h2[t][:].indirect(n3_t[:, c0 // 16 : c1 // 16]), rec[:], ALU.mult)
+            nc.sync.dma_start(out_rows[:, t, cols], y[:, t, :])
+
+        def planes(ci):
+            c0, c1 = CHUNKS[ci]
+            cols = slice(c0, c1)
+            y_il = new(f"y_il{ci}", [P, c1 - c0, PACK], BF16)
+            nc.vector.tensor_copy(y_il[:].rearrange("p (c i) t -> p c t i", i=4), ys[ci][:].rearrange("p t (c i) -> p c t i", i=4))
+            nc.vector.quantize_mx(o_w[:, cols].bitcast(FP8X4), o_s[:, cols], y_il[:].rearrange("p c t -> p (c t)"))
+            nc.sync.dma_start(words_of(out_1)[:, cols], o_w[:, cols].bitcast(I32))
+
+        nc.scalar.activation(ab[0][:], h2p[0][:], ACT.Abs)
+        for u in range(len(units) + 2):
+            if u + 1 < PACK:
+                nc.scalar.activation(ab[u + 1][:], h2p[u + 1][:], ACT.Abs)
+            if u < PACK:
+                nc.vector.tensor_copy(h2[u][:], h2p[u][:])
+            if u < len(units):
+                fetch(*units[u])
+            if 0 <= u - 1 < len(units):
+                root(*units[u - 1])
+            if 0 <= u - 2 < len(units):
+                finish(*units[u - 2])
+                if units[u - 2][1] == PACK - 1:
+                    planes(units[u - 2][0])
+        for q in range(4):
+            eng = nc.sync if q % 2 == 0 else nc.scalar
+            eng.dma_start(out_2[0, 4 * q : 4 * q + 4, :].bitcast(I32), o_s[32 * q : 32 * q + 4, :].bitcast(I32))

@@ -19,6 +19,7 @@ W = 384
 T = 1024
 G = 2048
 FLOPS = 3 * 2 * 512 * 512 * 512
+HALF = 256
 CHUNKS = [(0, 256), (256, 512)]
 
 
@@ -52,31 +53,34 @@ def tile_picked_pqmixkminnorm2_none_po_kernel(
         half = new("half", [P, 1], F32)
         nc.vector.memset(half[:], 0.5)
 
+        warm = new("warm", [P, 1], F32)
+        nc.scalar.activation(warm[:], half[:], ACT.Abs_reciprocal_sqrt, bias=half[:])
+
+        gn_t = new("gn_t", [P, PACK], F32)
+        nc.gpsimd.dma_start(gn_t[:], gn.rearrange("(p t) o -> p (t o)", t=PACK))
         k1_t = load_list("k1_t", k1)
         ds_win = new("ds_win", [P, G], U8, "early_a")
         nc.sync.dma_start(ds_win[:].bitcast(I32), spread(d_scales[0], 8))
-        dw_win = new("dw_win", [P, G], U32)
-        nc.sync.dma_start(dw_win[:].bitcast(I32), words_of(d_words))
         offs_t = load_list("offs_t", offs)
-        two_t = load_list("two_t", two)
-        n2_t = load_list("n2_t", n2)
-        n1_t = load_list("n1_t", n1)
-        xw_win = new("xw_win", [P, T], U32)
-        nc.sync.dma_start(xw_win[:].bitcast(I32), words_of(x_words))
-        n4_t = load_list("n4_t", n4)
-        n3_t = load_list("n3_t", n3)
         xs_win = new("xs_win", [P, T], U8)
         for j in range(4):
-            nc.gpsimd.dma_start(xs_win[j:P:4, :].bitcast(I32), spread(x_scales[0, j:16:4, :], 8))
-        gn_t = new("gn_t", [P, PACK], F32)
-        nc.gpsimd.dma_start(gn_t[:], gn.rearrange("(p t) o -> p (t o)", t=PACK))
+            nc.sync.dma_start(xs_win[j:P:4, :].bitcast(I32), spread(x_scales[0, j:16:4, :], 8))
+        dw_win = new("dw_win", [P, G], U32, "early_e")
+        nc.sync.dma_start(dw_win[:].bitcast(I32), words_of(d_words))
+        two_t = load_list("two_t", two)
+        n2_t = load_list("n2_t", n2)
+        xw_win = new("xw_win", [P, T], U32)
+        nc.sync.dma_start(xw_win[:].bitcast(I32), words_of(x_words))
+        n1_t = load_list("n1_t", n1)
+        n4_t = load_list("n4_t", n4)
+        n3_t = load_list("n3_t", n3)
 
         def deal(eng, dst, src):
             eng.tensor_copy(dst.rearrange("p (t m) -> p m t", t=PACK), src.rearrange("p (m t) -> p m t", t=PACK))
 
         ds_g = new("ds_g", [P, S], U8, "early_b")
         nc.vector.tensor_copy(ds_g[:], ds_win[:].indirect(k1_t[:]))
-        ds_d = new("ds_d", [P, S], U8)
+        ds_d = new("ds_d", [P, S], U8, "early_c")
         deal(nc.vector, ds_d[:], ds_g[:])
         for j in range(4):
             nc.scalar.dma_start(d_sc[j:P:32, :].bitcast(I32), ds_d[8 * j : P : 32, :].bitcast(I32))
@@ -87,68 +91,83 @@ def tile_picked_pqmixkminnorm2_none_po_kernel(
         for i, sc in enumerate((w1_scales, w2_scales)):
             for j in range(4):
                 nc.sync.dma_start(ws_raw[4 * i + j : P : 8, :].bitcast(I32), spread(sc[0, j:16:4, :], 4))
-        dw_g = new("dw_g", [P, S], U32)
-        nc.vector.tensor_copy(dw_g[:], dw_win[:].indirect(k1_t[:]))
-        xw_g = new("xw_g", [P, S], U32)
-        nc.vector.tensor_copy(xw_g[:], xw_win[:].indirect(offs_t[:]))
-        dw_d = new("dw_d", [P, S], U32)
-        deal(nc.vector, dw_d[:], dw_g[:])
         xs_g = new("xs_g", [P, S], U8)
         nc.vector.tensor_copy(xs_g[:], xs_win[:].indirect(offs_t[:]))
+        dw_g = new("dw_g", [P, S], U32, "early_d")
+        nc.vector.tensor_copy(dw_g[:], dw_win[:].indirect(k1_t[:]))
+        xw_g = [new("xw_g0", [P, HALF], U32, "early_e")]
+        nc.vector.tensor_copy(xw_g[0][:], xw_win[:].indirect(offs_t[:, 0:16]))
+        dw_d = new("dw_d", [P, S], U32)
+        deal(nc.vector, dw_d[:], dw_g[:])
+        xw_g.append(new("xw_g1", [P, HALF], U32, "early_d"))
+        nc.vector.tensor_copy(xw_g[1][:], xw_win[:].indirect(offs_t[:, 16:32]))
 
-        hp = [ps.tile([P, S], F32, name=f"hp{t}") for t in range(PACK)]
-        h2p = [ps.tile([P, S], F32, name=f"h2p{t}") for t in range(PACK)]
-        for t in range(PACK):
+        h = [new(f"h{t}", [P, S], F32) for t in range(PACK)]
+        hp = {}
+
+        for t, i in ((0, 0), (1, 0), (0, 1), (2, 0), (1, 1), (3, 0), (2, 1), (3, 1)):
             c = slice(P * t, P * (t + 1))
-            nc.tensor.matmul_mx(hp[t][:], lhsT=dw_d[:, c].bitcast(FP8X4), lhsT_scale=d_sc[:, c],
-                                rhs=xw_g[:].bitcast(FP8X4), rhs_scale=xs_g[:], start=True, stop=True)
+            hp[t, i] = ps.tile([P, HALF], F32, name=f"hp{t}_{i}", tag=f"bank{4 * i + t}")
+            nc.tensor.matmul_mx(hp[t, i][:], lhsT=dw_d[:, c].bitcast(FP8X4), lhsT_scale=d_sc[:, c],
+                                rhs=xw_g[i][:].bitcast(FP8X4), rhs_scale=xs_g[:, HALF * i : HALF * (i + 1)], start=True, stop=True)
 
-        x2w_g = new("x2w_g", [P, S], U32)
+        def h_out(t, i):
+            nc.scalar.activation(h[t][:, HALF * i : HALF * (i + 1)], hp[t, i][:], ACT.Copy, scale=0.0625)
+
+        x2w_g = new("x2w_g", [P, S], U32, "early_e")
         nc.vector.tensor_copy(x2w_g[:], xw_win[:].indirect(two_t[:]))
-        x2s_g = new("x2s_g", [P, S], U8)
+        x2s_g = new("x2s_g", [P, S], U8, "early_c")
         nc.vector.tensor_copy(x2s_g[:], xs_win[:].indirect(two_t[:]))
 
-        z_pl = new("z_pl", [P, PACK, S], BF16)
-        h = [new(f"h{t}", [P, S], F32) for t in range(PACK)]
+        w_d = new("w_d", [P, 2, S], U32)
+        for i in range(2):
+            deal(nc.vector, w_d[:, i, :], w_raw[:, i, :])
         nhp = [new(f"nhp{t}", [P, W], F32, f"mid_n{t}") for t in range(PACK)]
         a = [new(f"a{t}", [P, W], F32, f"mid_a{t}") for t in range(PACK)]
         ra = [new(f"ra{t}", [P, W], F32) for t in range(PACK)]
+        h_out(0, 0)
         for k in range(PACK + 2):
+            if k + 1 < PACK:
+                h_out(k + 1, 0)
             if k < PACK:
-                nc.scalar.activation(h[k][:], hp[k][:], ACT.Copy, scale=0.0625)
-            t = k - 1
+                h_out(k, 1)
+            t = k
             if 0 <= t < PACK:
                 nc.scalar.activation(nhp[t][:], h[t][:].indirect(n2_t[:]), ACT.Copy, scale=-0.5)
                 nc.vector.tensor_tensor(a[t][:], h[t][:].indirect(n1_t[:]), nhp[t][:], ALU.add)
-            t = k - 2
+            t = k - 1
             if 0 <= t < PACK:
                 nc.vector.scalar_tensor_tensor(ra[t][:], nhp[t][:], -1.0, a[t][:], ALU.mult, ALU.min)
         for t in range(2):
             nc.scalar.activation(h[t][:].indirect(n1_t[:]), ra[t][:], ACT.Copy)
-        nc.vector.tensor_copy(h[2][:].indirect(n1_t[:, 0:8]), ra[2][:, 0:128])
+        nc.vector.tensor_copy(h[2][:].indirect(n1_t[:, 0:6]), ra[2][:, 0:96])
         nc.vector.tensor_copy(h[3][:].indirect(n1_t[:]), ra[3][:])
-        nc.scalar.activation(h[2][:].indirect(n1_t[:, 8:24]), ra[2][:, 128:W], ACT.Copy)
-        w_d = new("w_d", [P, 2, S], U32, "mid_n3")
-        ws_d = new("ws_d", [P, S], U8, "mid_a3")
-        for i in range(2):
-            deal(nc.vector, w_d[:, i, :], w_raw[:, i, :])
+        nc.scalar.activation(h[2][:].indirect(n1_t[:, 6:24]), ra[2][:, 96:W], ACT.Copy)
+        ws_d = new("ws_d", [P, S], U8)
         deal(nc.vector, ws_d[:], ws_raw[:])
+        z_pl = new("z_pl", [P, PACK, S], BF16, "early_b")
+        h2p = {}
         for t in range(PACK):
-            c = slice(P * t, P * (t + 1))
-            nc.tensor.matmul_mx(h2p[t][:], lhsT=w_d[:, 1, c].bitcast(FP8X4), lhsT_scale=ws_d[4:P, c],
-                                rhs=x2w_g[:].bitcast(FP8X4), rhs_scale=x2s_g[:], start=True, stop=False)
-        for t in (0, 1, 3):
+            for i in range(2):
+                c = slice(P * t, P * (t + 1))
+                j = slice(HALF * i, HALF * (i + 1))
+                h2p[t, i] = ps.tile([P, HALF], F32, name=f"h2p{t}_{i}", tag=f"bank{4 * i + t}")
+                nc.tensor.matmul_mx(h2p[t, i][:], lhsT=w_d[:, 1, c].bitcast(FP8X4), lhsT_scale=ws_d[4:P, c],
+                                    rhs=x2w_g[:, j].bitcast(FP8X4), rhs_scale=x2s_g[:, j], start=True, stop=False)
+        for t in (0, 1, 3, 2):
             nc.vector.tensor_scalar(z_pl[:, t, :], h[t][:], gn_t[:, t : t + 1], None, ALU.mult)
-        nc.scalar.activation(z_pl[:, 2, :], h[2][:], ACT.Copy, scale=gn_t[:, 2:3])
-        z_il = new("z_il", [P, S, PACK], BF16)
-        nc.vector.tensor_copy(z_il[:].rearrange("p (c i) t -> p c t i", i=4), z_pl[:].rearrange("p t (c i) -> p c t i", i=4))
-        z_w = new("z_w", [P, S], U32)
-        z_s = new("z_s", [P, S], U8)
-        nc.vector.quantize_mx(z_w[:].bitcast(FP8X4), z_s[:], z_il[:].rearrange("p c t -> p (c t)"))
-        for t in range(PACK):
+        z_il = [new(f"z_il{i}", [P, HALF, PACK], BF16) for i in range(2)]
+        z_w = [new(f"z_w{i}", [P, HALF], U32) for i in range(2)]
+        z_s = [new(f"z_s{i}", [P, HALF], U8) for i in range(2)]
+        for i in range(2):
+            nc.vector.tensor_copy(z_il[i][:].rearrange("p (c i) t -> p c t i", i=4),
+                                  z_pl[:, :, HALF * i : HALF * (i + 1)].rearrange("p t (c i) -> p c t i", i=4))
+        for i in range(2):
+            nc.vector.quantize_mx(z_w[i][:].bitcast(FP8X4), z_s[i][:], z_il[i][:].rearrange("p c t -> p (c t)"))
+        for t, i in ((0, 0), (1, 0), (0, 1), (1, 1), (2, 0), (2, 1), (3, 0), (3, 1)):
             c = slice(P * t, P * (t + 1))
-            nc.tensor.matmul_mx(h2p[t][:], lhsT=w_d[:, 0, c].bitcast(FP8X4), lhsT_scale=ws_d[:, c],
-                                rhs=z_w[:].bitcast(FP8X4), rhs_scale=z_s[:], start=False, stop=True)
+            nc.tensor.matmul_mx(h2p[t, i][:], lhsT=w_d[:, 0, c].bitcast(FP8X4), lhsT_scale=ws_d[:, c],
+                                rhs=z_w[i][:].bitcast(FP8X4), rhs_scale=z_s[i][:], start=False, stop=True)
 
         h2 = [new(f"h2_{t}", [P, S], F32) for t in range(PACK)]
         ab = [new(f"ab{t}", [P, S], F32) for t in range(PACK)]
@@ -176,7 +195,10 @@ def tile_picked_pqmixkminnorm2_none_po_kernel(
             cols = slice(c0, c1)
             n = c1 - c0
             rec = new(f"rec{ci}_{t}", [P, n], F32)
-            nc.scalar.activation(rec[:], roots[ci, t][:], ACT.Square)
+            if ci == 0 and t < 2:
+                nc.vector.tensor_tensor(rec[:], roots[ci, t][:], roots[ci, t][:], ALU.mult)
+            else:
+                nc.scalar.activation(rec[:], roots[ci, t][:], ACT.Square)
             y = ys[ci]
             nc.vector.tensor_tensor(y[:, t, :], h2[t][:].indirect(n3_t[:, c0 // 16 : c1 // 16]), rec[:], ALU.mult)
             nc.sync.dma_start(out_rows[:, t, cols], y[:, t, :])
@@ -189,20 +211,38 @@ def tile_picked_pqmixkminnorm2_none_po_kernel(
             nc.vector.quantize_mx(o_w[:, cols].bitcast(FP8X4), o_s[:, cols], y_il[:].rearrange("p c t -> p (c t)"))
             nc.sync.dma_start(words_of(out_1)[:, cols], o_w[:, cols].bitcast(I32))
 
-        nc.scalar.activation(ab[0][:], h2p[0][:], ACT.Abs)
-        for u in range(len(units) + 2):
-            if u + 1 < PACK:
-                nc.scalar.activation(ab[u + 1][:], h2p[u + 1][:], ACT.Abs)
-            if u < PACK:
-                nc.vector.tensor_copy(h2[u][:], h2p[u][:])
+        def size_out(t, i):
+            nc.scalar.activation(ab[t][:, HALF * i : HALF * (i + 1)], h2p[t, i][:], ACT.Abs)
+
+        def h2_out(t):
+            for i in range(2):
+                nc.vector.tensor_copy(h2[t][:, HALF * i : HALF * (i + 1)], h2p[t, i][:])
+
+        size_out(0, 0)
+        size_out(0, 1)
+        size_out(1, 0)
+        h2_out(0)
+        h2_out(2)
+        fetch(*units[0])
+        size_out(1, 1)
+        h2_out(1)
+        h2_out(3)
+        for u in range(2):
+            fetch(*units[u + 1])
+            root(*units[u])
+            size_out(u + 2, 0)
+            size_out(u + 2, 1)
+            finish(*units[u])
+        fetch(*units[3])
+        root(*units[2])
+        for u in range(3, len(units) + 1):
+            if u + 1 < len(units):
+                fetch(*units[u + 1])
+            finish(*units[u - 1])
             if u < len(units):
-                fetch(*units[u])
-            if 0 <= u - 1 < len(units):
-                root(*units[u - 1])
-            if 0 <= u - 2 < len(units):
-                finish(*units[u - 2])
-                if units[u - 2][1] == PACK - 1:
-                    planes(units[u - 2][0])
+                root(*units[u])
+            if units[u - 1][1] == PACK - 1:
+                planes(units[u - 1][0])
         for q in range(4):
             eng = nc.sync if q % 2 == 0 else nc.scalar
             eng.dma_start(out_2[0, 4 * q : 4 * q + 4, :].bitcast(I32), o_s[32 * q : 32 * q + 4, :].bitcast(I32))

@@ -1,6 +1,7 @@
 from contextlib import ExitStack
 
 import concourse.mybir as mybir
+from concourse.masks import make_identity
 
 F32 = mybir.dt.float32
 BF16 = mybir.dt.bfloat16
@@ -48,76 +49,81 @@ def tile_picked_pqmixkminnorm2_none_po_kernel(
             nc.sync.dma_start(t[:], ap)
             return t
 
-        d_sc = new("d_sc", [P, S], U8)
-        nc.vector.memset(d_sc[:].bitcast(I32), 0)
+        pin = ctx.enter_context(tc.tile_pool(name="pin", bufs=1))
+
+        rows = new("rows", [P, 3 * S], U8)
+        nc.gpsimd.memset(rows[:].bitcast(I32), 0)
+        ident = new("ident", [P, P], F32)
+        make_identity(nc, ident[:])
         half = new("half", [P, 1], F32)
         nc.vector.memset(half[:], 0.5)
 
         warm = new("warm", [P, 1], F32)
         nc.scalar.activation(warm[:], half[:], ACT.Abs_reciprocal_sqrt, bias=half[:])
 
-        gn_t = new("gn_t", [P, PACK], F32)
-        nc.gpsimd.dma_start(gn_t[:], gn.rearrange("(p t) o -> p (t o)", t=PACK))
         k1_t = load_list("k1_t", k1)
-        ds_win = new("ds_win", [P, G], U8, "early_a")
+        ds_win = new("ds_win", [P, G], U8)
         nc.sync.dma_start(ds_win[:].bitcast(I32), spread(d_scales[0], 8))
         offs_t = load_list("offs_t", offs)
         xs_win = new("xs_win", [P, T], U8)
-        for j in range(4):
-            nc.sync.dma_start(xs_win[j:P:4, :].bitcast(I32), spread(x_scales[0, j:16:4, :], 8))
-        dw_win = new("dw_win", [P, G], U32, "early_e")
-        nc.sync.dma_start(dw_win[:].bitcast(I32), words_of(d_words))
+        nc.sync.dma_start(xs_win[:].bitcast(I32), spread(x_scales[0], 8))
         two_t = load_list("two_t", two)
         n2_t = load_list("n2_t", n2)
+        n1_t = load_list("n1_t", n1)
         xw_win = new("xw_win", [P, T], U32)
         nc.sync.dma_start(xw_win[:].bitcast(I32), words_of(x_words))
-        n1_t = load_list("n1_t", n1)
+        dw_win = new("dw_win", [P, G], U32, "early_e")
+        nc.sync.dma_start(dw_win[:].bitcast(I32), words_of(d_words))
         n4_t = load_list("n4_t", n4)
         n3_t = load_list("n3_t", n3)
+        gn_t = new("gn_t", [P, PACK], F32)
+        nc.sync.dma_start(gn_t[:], gn.rearrange("(p t) o -> p (t o)", t=PACK))
 
         def deal(eng, dst, src):
             eng.tensor_copy(dst.rearrange("p (t m) -> p m t", t=PACK), src.rearrange("p (m t) -> p m t", t=PACK))
 
-        ds_g = new("ds_g", [P, S], U8, "early_b")
-        nc.vector.tensor_copy(ds_g[:], ds_win[:].indirect(k1_t[:]))
-        ds_d = new("ds_d", [P, S], U8, "early_c")
-        deal(nc.vector, ds_d[:], ds_g[:])
-        for j in range(4):
-            nc.scalar.dma_start(d_sc[j:P:32, :].bitcast(I32), ds_d[8 * j : P : 32, :].bitcast(I32))
+        def move_rows(eng, dst, src):
+            for j in range(4):
+                eng.dma_start(dst[j:P:32, :].bitcast(I32), src[8 * j : P : 32, :].bitcast(I32))
+
+        sc_g = new("sc_g", [P, 2 * S], U8, "early_a")
+        nc.vector.tensor_copy(sc_g[:, 0:S], ds_win[:].indirect(k1_t[:]))
+        nc.vector.tensor_copy(sc_g[:, S : 2 * S], xs_win[:].indirect(offs_t[:]))
+        move_rows(nc.scalar, rows[:, 0 : 2 * S], sc_g[:])
+        xw_g = new("xw_g", [P, S], U32)
+        nc.vector.tensor_copy(xw_g[:], xw_win[:].indirect(offs_t[:]))
+        dw_g = pin.tile([P, S], U32, name="dw_g", align_bytes=64, offset=0)
+        nc.vector.tensor_copy(dw_g[:], dw_win[:].indirect(k1_t[:]))
+        dw_d = new("dw_d", [P, S], U32)
+        d_sc = new("d_sc", [P, S], U8, "early_e")
+        deal(nc.vector, dw_d[:], dw_g[:])
+        deal(nc.vector, d_sc[:], rows[:, 0:S])
+
         w_raw = new("w_raw", [P, 2, S], U32, "early_a")
         nc.sync.dma_start(w_raw[:, 0, :].bitcast(I32), words_of(w1_words))
         nc.sync.dma_start(w_raw[:, 1, :].bitcast(I32), words_of(w2_words))
-        ws_raw = new("ws_raw", [P, S], U8, "early_b")
+
+        h = [new(f"h{t}", [P, S], F32) for t in range(PACK)]
+        hp = []
+        for t in range(PACK):
+            c = slice(P * t, P * (t + 1))
+            hp.append(ps.tile([P, S], F32, name=f"hp{t}", tag=f"bank{t}"))
+            nc.tensor.matmul_mx(hp[t][:], lhsT=dw_d[:, c].bitcast(FP8X4), lhsT_scale=d_sc[:, c],
+                                rhs=xw_g[:].bitcast(FP8X4), rhs_scale=rows[:, S : 2 * S], start=True, stop=True)
+
+        def h_out(t):
+            nc.scalar.activation(h[t][:], hp[t][:], ACT.Copy, scale=0.0625)
+
+        x2w_g = pin.tile([P, S], U32, name="x2w_g", align_bytes=64, offset=1024)
+        nc.vector.tensor_copy(x2w_g[:], xw_win[:].indirect(two_t[:]))
+        x2s_r = pin.tile([P, S], U8, name="x2s_r", align_bytes=64, offset=0)
+        nc.vector.tensor_copy(x2s_r[:], xs_win[:].indirect(two_t[:]))
+        x2s_g = rows[:, 2 * S : 3 * S]
+        move_rows(nc.sync, x2s_g, x2s_r[:])
+        ws_raw = new("ws_raw", [P, S], U8, "early_e")
         for i, sc in enumerate((w1_scales, w2_scales)):
             for j in range(4):
                 nc.sync.dma_start(ws_raw[4 * i + j : P : 8, :].bitcast(I32), spread(sc[0, j:16:4, :], 4))
-        xs_g = new("xs_g", [P, S], U8)
-        nc.vector.tensor_copy(xs_g[:], xs_win[:].indirect(offs_t[:]))
-        dw_g = new("dw_g", [P, S], U32, "early_d")
-        nc.vector.tensor_copy(dw_g[:], dw_win[:].indirect(k1_t[:]))
-        xw_g = [new("xw_g0", [P, HALF], U32, "early_e")]
-        nc.vector.tensor_copy(xw_g[0][:], xw_win[:].indirect(offs_t[:, 0:16]))
-        dw_d = new("dw_d", [P, S], U32)
-        deal(nc.vector, dw_d[:], dw_g[:])
-        xw_g.append(new("xw_g1", [P, HALF], U32, "early_d"))
-        nc.vector.tensor_copy(xw_g[1][:], xw_win[:].indirect(offs_t[:, 16:32]))
-
-        h = [new(f"h{t}", [P, S], F32) for t in range(PACK)]
-        hp = {}
-
-        for t, i in ((0, 0), (1, 0), (0, 1), (2, 0), (1, 1), (3, 0), (2, 1), (3, 1)):
-            c = slice(P * t, P * (t + 1))
-            hp[t, i] = ps.tile([P, HALF], F32, name=f"hp{t}_{i}", tag=f"bank{4 * i + t}")
-            nc.tensor.matmul_mx(hp[t, i][:], lhsT=dw_d[:, c].bitcast(FP8X4), lhsT_scale=d_sc[:, c],
-                                rhs=xw_g[i][:].bitcast(FP8X4), rhs_scale=xs_g[:, HALF * i : HALF * (i + 1)], start=True, stop=True)
-
-        def h_out(t, i):
-            nc.scalar.activation(h[t][:, HALF * i : HALF * (i + 1)], hp[t, i][:], ACT.Copy, scale=0.0625)
-
-        x2w_g = new("x2w_g", [P, S], U32, "early_e")
-        nc.vector.tensor_copy(x2w_g[:], xw_win[:].indirect(two_t[:]))
-        x2s_g = new("x2s_g", [P, S], U8, "early_c")
-        nc.vector.tensor_copy(x2s_g[:], xs_win[:].indirect(two_t[:]))
 
         w_d = new("w_d", [P, 2, S], U32)
         for i in range(2):
@@ -125,12 +131,10 @@ def tile_picked_pqmixkminnorm2_none_po_kernel(
         nhp = [new(f"nhp{t}", [P, W], F32, f"mid_n{t}") for t in range(PACK)]
         a = [new(f"a{t}", [P, W], F32, f"mid_a{t}") for t in range(PACK)]
         ra = [new(f"ra{t}", [P, W], F32) for t in range(PACK)]
-        h_out(0, 0)
+        h_out(0)
         for k in range(PACK + 2):
             if k + 1 < PACK:
-                h_out(k + 1, 0)
-            if k < PACK:
-                h_out(k, 1)
+                h_out(k + 1)
             t = k
             if 0 <= t < PACK:
                 nc.scalar.activation(nhp[t][:], h[t][:].indirect(n2_t[:]), ACT.Copy, scale=-0.5)
@@ -145,7 +149,7 @@ def tile_picked_pqmixkminnorm2_none_po_kernel(
         nc.scalar.activation(h[2][:].indirect(n1_t[:, 6:24]), ra[2][:, 96:W], ACT.Copy)
         ws_d = new("ws_d", [P, S], U8)
         deal(nc.vector, ws_d[:], ws_raw[:])
-        z_pl = new("z_pl", [P, PACK, S], BF16, "early_b")
+        z_pl = new("z_pl", [P, PACK, S], BF16, "early_e")
         h2p = {}
         for t in range(PACK):
             for i in range(2):
@@ -176,29 +180,35 @@ def tile_picked_pqmixkminnorm2_none_po_kernel(
         o_s = new("o_s", [P, S], U8)
         units = [(ci, t) for ci in range(len(CHUNKS)) for t in range(PACK)]
         ys = [new(f"y{ci}", [P, PACK, c1 - c0], F32) for ci, (c0, c1) in enumerate(CHUNKS)]
-        dens, roots, recs = {}, {}, {}
+        dens, backs = {}, {}
 
         def fetch(ci, t):
             c0, c1 = CHUNKS[ci]
-            g4 = new(f"g4_{ci}_{t}", [P, c1 - c0], F32, "g4", 2)
-            nc.scalar.activation(g4[:], ab[t][:].indirect(n4_t[:, c0 // 16 : c1 // 16]), ACT.Copy)
-            dens[ci, t] = new(f"den{ci}_{t}", [P, c1 - c0], F32)
-            nc.vector.tensor_tensor(dens[ci, t][:], g4[:], ab[t][:, c0:c1], ALU.add)
+            g4 = new(f"g4_{ci}_{t}", [P, c1 - c0], F32)
+            looked_up = ab[t][:].indirect(n4_t[:, c0 // 16 : c1 // 16])
+            if ci == 0:
+                nc.vector.tensor_copy(g4[:], looked_up)
+            else:
+                nc.scalar.activation(g4[:], looked_up, ACT.Copy)
+            dens[ci, t] = ps.tile([P, c1 - c0], F32, name=f"den{ci}_{t}", tag=f"bank{t}")
+            for b in range(0, c1 - c0, P):
+                block = dens[ci, t][:, b : b + P]
+                nc.tensor.matmul(block, lhsT=ab[t][:, c0 + b : c0 + b + P], rhs=ident[:], is_transpose=True, start=True, stop=False)
+                nc.tensor.matmul(block, lhsT=g4[:, b : b + P], rhs=ident[:], is_transpose=True, start=False, stop=True)
 
         def root(ci, t):
             c0, c1 = CHUNKS[ci]
-            roots[ci, t] = new(f"r{ci}_{t}", [P, c1 - c0], F32)
-            nc.scalar.activation(roots[ci, t][:], dens[ci, t][:], ACT.Abs_reciprocal_sqrt, bias=half[:])
+            r = new(f"r{ci}_{t}", [P, c1 - c0], F32)
+            nc.scalar.activation(r[:], dens[ci, t][:], ACT.Abs_reciprocal_sqrt, bias=half[:])
+            backs[ci, t] = ps.tile([P, c1 - c0], F32, name=f"back{ci}_{t}", tag=f"bank{4 + t}")
+            for b in range(0, c1 - c0, P):
+                nc.tensor.transpose(backs[ci, t][:, b : b + P], r[:, b : b + P], ident[:])
 
         def finish(ci, t):
             c0, c1 = CHUNKS[ci]
             cols = slice(c0, c1)
-            n = c1 - c0
-            rec = new(f"rec{ci}_{t}", [P, n], F32)
-            if ci == 0 and t < 2:
-                nc.vector.tensor_tensor(rec[:], roots[ci, t][:], roots[ci, t][:], ALU.mult)
-            else:
-                nc.scalar.activation(rec[:], roots[ci, t][:], ACT.Square)
+            rec = new(f"rec{ci}_{t}", [P, c1 - c0], F32)
+            nc.scalar.activation(rec[:], backs[ci, t][:], ACT.Square)
             y = ys[ci]
             nc.vector.tensor_tensor(y[:, t, :], h2[t][:].indirect(n3_t[:, c0 // 16 : c1 // 16]), rec[:], ALU.mult)
             nc.sync.dma_start(out_rows[:, t, cols], y[:, t, :])
@@ -211,38 +221,24 @@ def tile_picked_pqmixkminnorm2_none_po_kernel(
             nc.vector.quantize_mx(o_w[:, cols].bitcast(FP8X4), o_s[:, cols], y_il[:].rearrange("p c t -> p (c t)"))
             nc.sync.dma_start(words_of(out_1)[:, cols], o_w[:, cols].bitcast(I32))
 
-        def size_out(t, i):
-            nc.scalar.activation(ab[t][:, HALF * i : HALF * (i + 1)], h2p[t, i][:], ACT.Abs)
-
-        def h2_out(t):
+        def leave_banks(t):
             for i in range(2):
+                nc.scalar.activation(ab[t][:, HALF * i : HALF * (i + 1)], h2p[t, i][:], ACT.Abs)
+            for i in (1, 0):
                 nc.vector.tensor_copy(h2[t][:, HALF * i : HALF * (i + 1)], h2p[t, i][:])
 
-        size_out(0, 0)
-        size_out(0, 1)
-        size_out(1, 0)
-        h2_out(0)
-        h2_out(2)
-        fetch(*units[0])
-        size_out(1, 1)
-        h2_out(1)
-        h2_out(3)
-        for u in range(2):
-            fetch(*units[u + 1])
-            root(*units[u])
-            size_out(u + 2, 0)
-            size_out(u + 2, 1)
-            finish(*units[u])
-        fetch(*units[3])
-        root(*units[2])
-        for u in range(3, len(units) + 1):
-            if u + 1 < len(units):
-                fetch(*units[u + 1])
-            finish(*units[u - 1])
-            if u < len(units):
-                root(*units[u])
-            if units[u - 1][1] == PACK - 1:
-                planes(units[u - 1][0])
+        leave_banks(0)
+        for step in range(len(units) + 2):
+            if step + 1 < PACK:
+                leave_banks(step + 1)
+            if step < len(units):
+                fetch(*units[step])
+            if 0 <= step - 1 < len(units):
+                root(*units[step - 1])
+            if 0 <= step - 2:
+                finish(*units[step - 2])
+                if units[step - 2][1] == PACK - 1:
+                    planes(units[step - 2][0])
         for q in range(4):
             eng = nc.sync if q % 2 == 0 else nc.scalar
             eng.dma_start(out_2[0, 4 * q : 4 * q + 4, :].bitcast(I32), o_s[32 * q : 32 * q + 4, :].bitcast(I32))

@@ -19,9 +19,11 @@ S = 512
 W = 384
 T = 1024
 G = 2048
+HALF = S // 2
+PER_COLUMN = 16
+VECTOR_ENTRIES = 96
+SCALAR_FROM = 384
 FLOPS = 3 * 2 * 512 * 512 * 512
-HALF = 256
-CHUNKS = [(0, 256), (256, 512)]
 
 
 def tile_picked_pqmixkminnorm2_none_po_kernel(
@@ -37,19 +39,22 @@ def tile_picked_pqmixkminnorm2_none_po_kernel(
         sb = ctx.enter_context(tc.tile_pool(name="sb", bufs=1))
         ps = ctx.enter_context(tc.psum_pool(name="ps", bufs=1))
 
-        def new(name, shape, dtype, tag=None, bufs=1):
-            return sb.tile(shape, dtype, name=name, tag=tag or name, bufs=bufs, align_bytes=64)
+        def new(name, shape, dtype, tag=None):
+            return sb.tile(shape, dtype, name=name, tag=tag or name, bufs=1, align_bytes=64)
 
-        def spread(rows, times):
-            rows = rows.bitcast(I32)
-            return rows.unsqueeze(1).broadcast_to([rows.shape[0], times, rows.shape[1]])
+        def spread(scale_rows, times):
+            as_words = scale_rows.bitcast(I32)
+            return as_words.unsqueeze(1).broadcast_to([as_words.shape[0], times, as_words.shape[1]])
 
         def load_list(name, ap):
-            t = new(name, list(ap.shape), U16)
-            nc.sync.dma_start(t[:], ap)
-            return t
+            list_tile = new(name, list(ap.shape), U16)
+            nc.sync.dma_start(list_tile[:], ap)
+            return list_tile
 
-        pin = ctx.enter_context(tc.tile_pool(name="pin", bufs=1))
+        def entries(list_tile, first, end):
+            return list_tile[:, first // PER_COLUMN : end // PER_COLUMN]
+
+        placed = ctx.enter_context(tc.tile_pool(name="placed", bufs=1))
 
         rows = new("rows", [P, 3 * S], U8)
         nc.gpsimd.memset(rows[:].bitcast(I32), 0)
@@ -61,45 +66,45 @@ def tile_picked_pqmixkminnorm2_none_po_kernel(
         warm = new("warm", [P, 1], F32)
         nc.scalar.activation(warm[:], half[:], ACT.Abs_reciprocal_sqrt, bias=half[:])
 
-        k1_t = load_list("k1_t", k1)
-        ds_win = new("ds_win", [P, G], U8)
-        nc.sync.dma_start(ds_win[:].bitcast(I32), spread(d_scales[0], 8))
         offs_t = load_list("offs_t", offs)
         xs_win = new("xs_win", [P, T], U8)
         nc.sync.dma_start(xs_win[:].bitcast(I32), spread(x_scales[0], 8))
+        k1_t = load_list("k1_t", k1)
+        ds_win = new("ds_win", [P, G], U8)
+        nc.sync.dma_start(ds_win[:].bitcast(I32), spread(d_scales[0], 8))
         two_t = load_list("two_t", two)
         n2_t = load_list("n2_t", n2)
         n1_t = load_list("n1_t", n1)
         xw_win = new("xw_win", [P, T], U32)
         nc.sync.dma_start(xw_win[:].bitcast(I32), words_of(x_words))
-        dw_win = new("dw_win", [P, G], U32, "early_e")
+        dw_win = new("dw_win", [P, G], U32, "after_dw_win")
         nc.sync.dma_start(dw_win[:].bitcast(I32), words_of(d_words))
         n4_t = load_list("n4_t", n4)
         n3_t = load_list("n3_t", n3)
         gn_t = new("gn_t", [P, PACK], F32)
         nc.sync.dma_start(gn_t[:], gn.rearrange("(p t) o -> p (t o)", t=PACK))
 
-        def deal(eng, dst, src):
-            eng.tensor_copy(dst.rearrange("p (t m) -> p m t", t=PACK), src.rearrange("p (m t) -> p m t", t=PACK))
+        def deal(dst, src):
+            nc.vector.tensor_copy(dst.rearrange("p (t m) -> p m t", t=PACK), src.rearrange("p (m t) -> p m t", t=PACK))
 
         def move_rows(eng, dst, src):
             for j in range(4):
                 eng.dma_start(dst[j:P:32, :].bitcast(I32), src[8 * j : P : 32, :].bitcast(I32))
 
-        sc_g = new("sc_g", [P, 2 * S], U8, "early_a")
-        nc.vector.tensor_copy(sc_g[:, 0:S], ds_win[:].indirect(k1_t[:]))
+        sc_g = new("sc_g", [P, 2 * S], U8, "after_sc_g")
         nc.vector.tensor_copy(sc_g[:, S : 2 * S], xs_win[:].indirect(offs_t[:]))
+        nc.vector.tensor_copy(sc_g[:, 0:S], ds_win[:].indirect(k1_t[:]))
         move_rows(nc.scalar, rows[:, 0 : 2 * S], sc_g[:])
         xw_g = new("xw_g", [P, S], U32)
         nc.vector.tensor_copy(xw_g[:], xw_win[:].indirect(offs_t[:]))
-        dw_g = pin.tile([P, S], U32, name="dw_g", align_bytes=64, offset=0)
+        dw_g = placed.tile([P, S], U32, name="dw_g", align_bytes=64, offset=0)
         nc.vector.tensor_copy(dw_g[:], dw_win[:].indirect(k1_t[:]))
         dw_d = new("dw_d", [P, S], U32)
-        d_sc = new("d_sc", [P, S], U8, "early_e")
-        deal(nc.vector, dw_d[:], dw_g[:])
-        deal(nc.vector, d_sc[:], rows[:, 0:S])
+        d_sc = new("d_sc", [P, S], U8, "after_dw_win")
+        deal(dw_d[:], dw_g[:])
+        deal(d_sc[:], rows[:, 0:S])
 
-        w_raw = new("w_raw", [P, 2, S], U32, "early_a")
+        w_raw = new("w_raw", [P, 2, S], U32, "after_sc_g")
         nc.sync.dma_start(w_raw[:, 0, :].bitcast(I32), words_of(w1_words))
         nc.sync.dma_start(w_raw[:, 1, :].bitcast(I32), words_of(w2_words))
 
@@ -114,131 +119,141 @@ def tile_picked_pqmixkminnorm2_none_po_kernel(
         def h_out(t):
             nc.scalar.activation(h[t][:], hp[t][:], ACT.Copy, scale=0.0625)
 
-        x2w_g = pin.tile([P, S], U32, name="x2w_g", align_bytes=64, offset=1024)
+        x2w_g = placed.tile([P, S], U32, name="x2w_g", align_bytes=64, offset=1024)
         nc.vector.tensor_copy(x2w_g[:], xw_win[:].indirect(two_t[:]))
-        x2s_r = pin.tile([P, S], U8, name="x2s_r", align_bytes=64, offset=0)
-        nc.vector.tensor_copy(x2s_r[:], xs_win[:].indirect(two_t[:]))
-        x2s_g = rows[:, 2 * S : 3 * S]
-        move_rows(nc.sync, x2s_g, x2s_r[:])
-        ws_raw = new("ws_raw", [P, S], U8, "early_e")
-        for i, sc in enumerate((w1_scales, w2_scales)):
+        x2s_g = placed.tile([P, S], U8, name="x2s_g", align_bytes=64, offset=0)
+        nc.vector.tensor_copy(x2s_g[:], xs_win[:].indirect(two_t[:]))
+        x2_sc = rows[:, 2 * S : 3 * S]
+        move_rows(nc.sync, x2_sc, x2s_g[:])
+        ws_raw = new("ws_raw", [P, S], U8, "after_dw_win")
+        for i, scales in enumerate((w1_scales, w2_scales)):
             for j in range(4):
-                nc.sync.dma_start(ws_raw[4 * i + j : P : 8, :].bitcast(I32), spread(sc[0, j:16:4, :], 4))
+                nc.sync.dma_start(ws_raw[4 * i + j : P : 8, :].bitcast(I32), spread(scales[0, j:16:4, :], 4))
 
         w_d = new("w_d", [P, 2, S], U32)
         for i in range(2):
-            deal(nc.vector, w_d[:, i, :], w_raw[:, i, :])
-        nhp = [new(f"nhp{t}", [P, W], F32, f"mid_n{t}") for t in range(PACK)]
-        a = [new(f"a{t}", [P, W], F32, f"mid_a{t}") for t in range(PACK)]
+            deal(w_d[:, i, :], w_raw[:, i, :])
+
+        minus_half_pa = [new(f"minus_half_pa{t}", [P, W], F32) for t in range(PACK)]
+        old_less = [new(f"old_less{t}", [P, W], F32) for t in range(PACK)]
         ra = [new(f"ra{t}", [P, W], F32) for t in range(PACK)]
         h_out(0)
-        for k in range(PACK + 2):
+        for k in range(PACK + 1):
             if k + 1 < PACK:
                 h_out(k + 1)
-            t = k
-            if 0 <= t < PACK:
-                nc.scalar.activation(nhp[t][:], h[t][:].indirect(n2_t[:]), ACT.Copy, scale=-0.5)
-                nc.vector.tensor_tensor(a[t][:], h[t][:].indirect(n1_t[:]), nhp[t][:], ALU.add)
-            t = k - 1
-            if 0 <= t < PACK:
-                nc.vector.scalar_tensor_tensor(ra[t][:], nhp[t][:], -1.0, a[t][:], ALU.mult, ALU.min)
+            if k < PACK:
+                nc.scalar.activation(minus_half_pa[k][:], h[k][:].indirect(n2_t[:]), ACT.Copy, scale=-0.5)
+                nc.vector.tensor_tensor(old_less[k][:], h[k][:].indirect(n1_t[:]), minus_half_pa[k][:], ALU.add)
+            if k >= 1:
+                nc.vector.scalar_tensor_tensor(ra[k - 1][:], minus_half_pa[k - 1][:], -1.0, old_less[k - 1][:], ALU.mult, ALU.min)
+
         for t in range(2):
             nc.scalar.activation(h[t][:].indirect(n1_t[:]), ra[t][:], ACT.Copy)
-        nc.vector.tensor_copy(h[2][:].indirect(n1_t[:, 0:6]), ra[2][:, 0:96])
+        nc.vector.tensor_copy(h[2][:].indirect(entries(n1_t, 0, VECTOR_ENTRIES)), ra[2][:, 0:VECTOR_ENTRIES])
         nc.vector.tensor_copy(h[3][:].indirect(n1_t[:]), ra[3][:])
-        nc.scalar.activation(h[2][:].indirect(n1_t[:, 6:24]), ra[2][:, 96:W], ACT.Copy)
+        nc.scalar.activation(h[2][:].indirect(entries(n1_t, VECTOR_ENTRIES, W)), ra[2][:, VECTOR_ENTRIES:W], ACT.Copy)
         ws_d = new("ws_d", [P, S], U8)
-        deal(nc.vector, ws_d[:], ws_raw[:])
-        z_pl = new("z_pl", [P, PACK, S], BF16, "early_e")
+        deal(ws_d[:], ws_raw[:])
+
+        z_tiles = new("z_tiles", [P, PACK, S], BF16, "after_dw_win")
         h2p = {}
         for t in range(PACK):
             for i in range(2):
                 c = slice(P * t, P * (t + 1))
-                j = slice(HALF * i, HALF * (i + 1))
-                h2p[t, i] = ps.tile([P, HALF], F32, name=f"h2p{t}_{i}", tag=f"bank{4 * i + t}")
+                cols = slice(HALF * i, HALF * (i + 1))
+                h2p[t, i] = ps.tile([P, HALF], F32, name=f"h2p{t}_{i}", tag=f"bank{PACK * i + t}")
                 nc.tensor.matmul_mx(h2p[t, i][:], lhsT=w_d[:, 1, c].bitcast(FP8X4), lhsT_scale=ws_d[4:P, c],
-                                    rhs=x2w_g[:, j].bitcast(FP8X4), rhs_scale=x2s_g[:, j], start=True, stop=False)
-        for t in (0, 1, 3, 2):
-            nc.vector.tensor_scalar(z_pl[:, t, :], h[t][:], gn_t[:, t : t + 1], None, ALU.mult)
+                                    rhs=x2w_g[:, cols].bitcast(FP8X4), rhs_scale=x2_sc[:, cols], start=True, stop=False)
+        for t in (0, 1, 3):
+            nc.vector.tensor_scalar(z_tiles[:, t, :], h[t][:], gn_t[:, t : t + 1], None, ALU.mult)
+        for cols in (slice(0, HALF), slice(HALF, SCALAR_FROM)):
+            nc.vector.tensor_scalar(z_tiles[:, 2, cols], h[2][:, cols], gn_t[:, 2:3], None, ALU.mult)
+        nc.scalar.activation(z_tiles[:, 2, SCALAR_FROM:S], h[2][:, SCALAR_FROM:S], ACT.Copy, scale=gn_t[:, 2:3])
+
+        def interleave_on_vector(dst, src):
+            nc.vector.tensor_copy(dst.rearrange("p (c i) t -> p c t i", i=4), src.rearrange("p t (c i) -> p c t i", i=4))
+
+        def interleave_on_scalar(dst, src):
+            nc.scalar.copy(dst, src.rearrange("p t c -> p c t"))
+
         z_il = [new(f"z_il{i}", [P, HALF, PACK], BF16) for i in range(2)]
         z_w = [new(f"z_w{i}", [P, HALF], U32) for i in range(2)]
         z_s = [new(f"z_s{i}", [P, HALF], U8) for i in range(2)]
-        for i in range(2):
-            nc.vector.tensor_copy(z_il[i][:].rearrange("p (c i) t -> p c t i", i=4),
-                                  z_pl[:, :, HALF * i : HALF * (i + 1)].rearrange("p t (c i) -> p c t i", i=4))
+        interleave_on_vector(z_il[0][:], z_tiles[:, :, 0:HALF])
+        interleave_on_scalar(z_il[1][:, SCALAR_FROM - HALF : HALF, :], z_tiles[:, :, SCALAR_FROM:S])
+        interleave_on_vector(z_il[1][:, 0 : SCALAR_FROM - HALF, :], z_tiles[:, :, HALF:SCALAR_FROM])
         for i in range(2):
             nc.vector.quantize_mx(z_w[i][:].bitcast(FP8X4), z_s[i][:], z_il[i][:].rearrange("p c t -> p (c t)"))
-        for t, i in ((0, 0), (1, 0), (0, 1), (1, 1), (2, 0), (2, 1), (3, 0), (3, 1)):
+        for t, i in [(0, 0), (1, 0), (0, 1), (1, 1)] + [(t, i) for t in (2, 3) for i in range(2)]:
             c = slice(P * t, P * (t + 1))
             nc.tensor.matmul_mx(h2p[t, i][:], lhsT=w_d[:, 0, c].bitcast(FP8X4), lhsT_scale=ws_d[:, c],
                                 rhs=z_w[i][:].bitcast(FP8X4), rhs_scale=z_s[i][:], start=False, stop=True)
 
         h2 = [new(f"h2_{t}", [P, S], F32) for t in range(PACK)]
-        ab = [new(f"ab{t}", [P, S], F32) for t in range(PACK)]
+        size = [new(f"size{t}", [P, S], F32) for t in range(PACK)]
         out_rows = out_0.rearrange("(p t) c -> p t c", t=PACK)
         o_w = new("o_w", [P, S], U32)
         o_s = new("o_s", [P, S], U8)
-        units = [(ci, t) for ci in range(len(CHUNKS)) for t in range(PACK)]
-        ys = [new(f"y{ci}", [P, PACK, c1 - c0], F32) for ci, (c0, c1) in enumerate(CHUNKS)]
-        dens, backs = {}, {}
+        pieces = [(i, t) for i in range(2) for t in range(PACK)]
+        y = [new(f"y{i}", [P, PACK, HALF], F32) for i in range(2)]
+        sums, roots = {}, {}
 
-        def fetch(ci, t):
-            c0, c1 = CHUNKS[ci]
-            g4 = new(f"g4_{ci}_{t}", [P, c1 - c0], F32)
-            looked_up = ab[t][:].indirect(n4_t[:, c0 // 16 : c1 // 16])
-            if ci == 0:
-                nc.vector.tensor_copy(g4[:], looked_up)
+        def add_sizes(i, t):
+            c0 = HALF * i
+            fetched = new(f"fetched{i}_{t}", [P, HALF], F32)
+            looked_up = size[t][:].indirect(entries(n4_t, c0, c0 + HALF))
+            if i == 0:
+                nc.vector.tensor_copy(fetched[:], looked_up)
             else:
-                nc.scalar.activation(g4[:], looked_up, ACT.Copy)
-            dens[ci, t] = ps.tile([P, c1 - c0], F32, name=f"den{ci}_{t}", tag=f"bank{t}")
-            for b in range(0, c1 - c0, P):
-                block = dens[ci, t][:, b : b + P]
-                nc.tensor.matmul(block, lhsT=ab[t][:, c0 + b : c0 + b + P], rhs=ident[:], is_transpose=True, start=True, stop=False)
-                nc.tensor.matmul(block, lhsT=g4[:, b : b + P], rhs=ident[:], is_transpose=True, start=False, stop=True)
+                nc.scalar.activation(fetched[:], looked_up, ACT.Copy)
+            sums[i, t] = ps.tile([P, HALF], F32, name=f"sum{i}_{t}", tag=f"bank{t}")
+            for b in range(0, HALF, P):
+                block = sums[i, t][:, b : b + P]
+                nc.tensor.matmul(block, lhsT=size[t][:, c0 + b : c0 + b + P], rhs=ident[:], is_transpose=True, start=True, stop=False)
+                nc.tensor.matmul(block, lhsT=fetched[:, b : b + P], rhs=ident[:], is_transpose=True, start=False, stop=True)
 
-        def root(ci, t):
-            c0, c1 = CHUNKS[ci]
-            r = new(f"r{ci}_{t}", [P, c1 - c0], F32)
-            nc.scalar.activation(r[:], dens[ci, t][:], ACT.Abs_reciprocal_sqrt, bias=half[:])
-            backs[ci, t] = ps.tile([P, c1 - c0], F32, name=f"back{ci}_{t}", tag=f"bank{4 + t}")
-            for b in range(0, c1 - c0, P):
-                nc.tensor.transpose(backs[ci, t][:, b : b + P], r[:, b : b + P], ident[:])
+        def inverse_root(i, t):
+            root_t = new(f"root_t{i}_{t}", [P, HALF], F32)
+            nc.scalar.activation(root_t[:], sums[i, t][:], ACT.Abs_reciprocal_sqrt, bias=half[:])
+            roots[i, t] = ps.tile([P, HALF], F32, name=f"root{i}_{t}", tag=f"bank{PACK + t}")
+            for b in range(0, HALF, P):
+                nc.tensor.transpose(roots[i, t][:, b : b + P], root_t[:, b : b + P], ident[:])
 
-        def finish(ci, t):
-            c0, c1 = CHUNKS[ci]
-            cols = slice(c0, c1)
-            rec = new(f"rec{ci}_{t}", [P, c1 - c0], F32)
-            nc.scalar.activation(rec[:], backs[ci, t][:], ACT.Square)
-            y = ys[ci]
-            nc.vector.tensor_tensor(y[:, t, :], h2[t][:].indirect(n3_t[:, c0 // 16 : c1 // 16]), rec[:], ALU.mult)
-            nc.sync.dma_start(out_rows[:, t, cols], y[:, t, :])
-
-        def planes(ci):
-            c0, c1 = CHUNKS[ci]
-            cols = slice(c0, c1)
-            y_il = new(f"y_il{ci}", [P, c1 - c0, PACK], BF16)
-            nc.vector.tensor_copy(y_il[:].rearrange("p (c i) t -> p c t i", i=4), ys[ci][:].rearrange("p t (c i) -> p c t i", i=4))
-            nc.vector.quantize_mx(o_w[:, cols].bitcast(FP8X4), o_s[:, cols], y_il[:].rearrange("p c t -> p (c t)"))
-            nc.sync.dma_start(words_of(out_1)[:, cols], o_w[:, cols].bitcast(I32))
+        def divide(i, t):
+            c0 = HALF * i
+            inverse = new(f"inverse{i}_{t}", [P, HALF], F32)
+            nc.scalar.activation(inverse[:], roots[i, t][:], ACT.Square)
+            width = P if (i, t) == pieces[-1] else HALF
+            for b in range(0, HALF, width):
+                looked_up = h2[t][:].indirect(entries(n3_t, c0 + b, c0 + b + width))
+                nc.vector.tensor_tensor(y[i][:, t, b : b + width], looked_up, inverse[:, b : b + width], ALU.mult)
+            nc.sync.dma_start(out_rows[:, t, c0 : c0 + HALF], y[i][:, t, :])
 
         def leave_banks(t):
             for i in range(2):
-                nc.scalar.activation(ab[t][:, HALF * i : HALF * (i + 1)], h2p[t, i][:], ACT.Abs)
+                nc.scalar.activation(size[t][:, HALF * i : HALF * (i + 1)], h2p[t, i][:], ACT.Abs)
             for i in (1, 0):
                 nc.vector.tensor_copy(h2[t][:, HALF * i : HALF * (i + 1)], h2p[t, i][:])
 
         leave_banks(0)
-        for step in range(len(units) + 2):
+        for step in range(len(pieces) + 2):
             if step + 1 < PACK:
                 leave_banks(step + 1)
-            if step < len(units):
-                fetch(*units[step])
-            if 0 <= step - 1 < len(units):
-                root(*units[step - 1])
-            if 0 <= step - 2:
-                finish(*units[step - 2])
-                if units[step - 2][1] == PACK - 1:
-                    planes(units[step - 2][0])
+            if step < len(pieces):
+                add_sizes(*pieces[step])
+            if 1 <= step <= len(pieces):
+                inverse_root(*pieces[step - 1])
+            if step >= 2:
+                divide(*pieces[step - 2])
+
+        y_il = [new("y_il0", [P, HALF, PACK], BF16, "root_t1_3")]
+        interleave_on_scalar(y_il[0][:], y[0][:])
+        for b in (0, P):
+            y_il.append(new(f"y_il1_{b}", [P, P, PACK], BF16))
+            interleave_on_vector(y_il[-1][:], y[1][:, :, b : b + P])
+        for part, cols in zip(y_il, (slice(0, HALF), slice(HALF, HALF + P), slice(HALF + P, S))):
+            nc.vector.quantize_mx(o_w[:, cols].bitcast(FP8X4), o_s[:, cols], part[:].rearrange("p c t -> p (c t)"))
+            nc.sync.dma_start(words_of(out_1)[:, cols], o_w[:, cols].bitcast(I32))
         for q in range(4):
             eng = nc.sync if q % 2 == 0 else nc.scalar
             eng.dma_start(out_2[0, 4 * q : 4 * q + 4, :].bitcast(I32), o_s[32 * q : 32 * q + 4, :].bitcast(I32))

from contextlib import ExitStack

import concourse.mybir as mybir
from concourse.masks import make_identity

F32 = mybir.dt.float32
BF16 = mybir.dt.bfloat16
I32 = mybir.dt.int32
U32 = mybir.dt.uint32
U16 = mybir.dt.uint16
U8 = mybir.dt.uint8
FP8X4 = mybir.dt.float8_e4m3fn_x4
ALU = mybir.AluOpType
ACT = mybir.ActivationFunctionType

P = 128
PACK = 4
S = 512
W = 384
T = 1024
G = 2048
HALF = S // 2
PER_COLUMN = 16
VECTOR_ENTRIES = 96
SCALAR_FROM = 384
FLOPS = 3 * 2 * 512 * 512 * 512


def tile_picked_pqmixkminnorm2_none_po_kernel(
    tc, x_words, x_scales, d_words, d_scales, gn, w1_words, w1_scales, w2_words, w2_scales,
    offs, k1, n1, n2, two, n3, n4, out_0, out_1, out_2,
):
    nc = tc.nc

    def words_of(ap):
        return ap[0].rearrange("p c r -> p (c r)").bitcast(I32)

    with ExitStack() as ctx:
        sb = ctx.enter_context(tc.tile_pool(name="sb", bufs=1))
        ps = ctx.enter_context(tc.psum_pool(name="ps", bufs=1))

        def new(name, shape, dtype, tag=None):
            return sb.tile(shape, dtype, name=name, tag=tag or name, bufs=1, align_bytes=64)

        def spread(scale_rows, times):
            as_words = scale_rows.bitcast(I32)
            return as_words.unsqueeze(1).broadcast_to([as_words.shape[0], times, as_words.shape[1]])

        def load_list(name, ap):
            list_tile = new(name, list(ap.shape), U16)
            nc.sync.dma_start(list_tile[:], ap)
            return list_tile

        def entries(list_tile, first, end):
            return list_tile[:, first // PER_COLUMN : end // PER_COLUMN]

        placed = ctx.enter_context(tc.tile_pool(name="placed", bufs=1))

        rows = new("rows", [P, 3 * S], U8)
        nc.gpsimd.memset(rows[:].bitcast(I32), 0)
        ident = new("ident", [P, P], F32)
        make_identity(nc, ident[:])
        half = new("half", [P, 1], F32)
        nc.vector.memset(half[:], 0.5)

        warm = new("warm", [P, 1], F32)
        nc.scalar.activation(warm[:], half[:], ACT.Abs_reciprocal_sqrt, bias=half[:])

        offs_t = load_list("offs_t", offs)
        xs_win = new("xs_win", [P, T], U8)
        nc.sync.dma_start(xs_win[:].bitcast(I32), spread(x_scales[0], 8))
        k1_t = load_list("k1_t", k1)
        ds_win = new("ds_win", [P, G], U8)
        nc.sync.dma_start(ds_win[:].bitcast(I32), spread(d_scales[0], 8))
        two_t = load_list("two_t", two)
        n2_t = load_list("n2_t", n2)
        n1_t = load_list("n1_t", n1)
        xw_win = new("xw_win", [P, T], U32)
        nc.sync.dma_start(xw_win[:].bitcast(I32), words_of(x_words))
        dw_win = new("dw_win", [P, G], U32, "after_dw_win")
        nc.sync.dma_start(dw_win[:].bitcast(I32), words_of(d_words))
        n4_t = load_list("n4_t", n4)
        n3_t = load_list("n3_t", n3)
        gn_t = new("gn_t", [P, PACK], F32)
        nc.sync.dma_start(gn_t[:], gn.rearrange("(p t) o -> p (t o)", t=PACK))

        def deal(dst, src):
            nc.vector.tensor_copy(dst.rearrange("p (t m) -> p m t", t=PACK), src.rearrange("p (m t) -> p m t", t=PACK))

        def move_rows(eng, dst, src):
            for j in range(4):
                eng.dma_start(dst[j:P:32, :].bitcast(I32), src[8 * j : P : 32, :].bitcast(I32))

        sc_g = new("sc_g", [P, 2 * S], U8, "after_sc_g")
        nc.vector.tensor_copy(sc_g[:, S : 2 * S], xs_win[:].indirect(offs_t[:]))
        nc.vector.tensor_copy(sc_g[:, 0:S], ds_win[:].indirect(k1_t[:]))
        move_rows(nc.scalar, rows[:, 0 : 2 * S], sc_g[:])
        xw_g = new("xw_g", [P, S], U32)
        nc.vector.tensor_copy(xw_g[:], xw_win[:].indirect(offs_t[:]))
        dw_g = placed.tile([P, S], U32, name="dw_g", align_bytes=64, offset=0)
        nc.vector.tensor_copy(dw_g[:], dw_win[:].indirect(k1_t[:]))
        dw_d = new("dw_d", [P, S], U32)
        d_sc = new("d_sc", [P, S], U8, "after_dw_win")
        deal(dw_d[:], dw_g[:])
        deal(d_sc[:], rows[:, 0:S])

        w_raw = new("w_raw", [P, 2, S], U32, "after_sc_g")
        nc.sync.dma_start(w_raw[:, 0, :].bitcast(I32), words_of(w1_words))
        nc.sync.dma_start(w_raw[:, 1, :].bitcast(I32), words_of(w2_words))

        h = [new(f"h{t}", [P, S], F32) for t in range(PACK)]
        hp = []
        for t in range(PACK):
            c = slice(P * t, P * (t + 1))
            hp.append(ps.tile([P, S], F32, name=f"hp{t}", tag=f"bank{t}"))
            nc.tensor.matmul_mx(hp[t][:], lhsT=dw_d[:, c].bitcast(FP8X4), lhsT_scale=d_sc[:, c],
                                rhs=xw_g[:].bitcast(FP8X4), rhs_scale=rows[:, S : 2 * S], start=True, stop=True)

        def h_out(t):
            nc.scalar.activation(h[t][:], hp[t][:], ACT.Copy, scale=0.0625)

        x2w_g = placed.tile([P, S], U32, name="x2w_g", align_bytes=64, offset=1024)
        nc.vector.tensor_copy(x2w_g[:], xw_win[:].indirect(two_t[:]))
        x2s_g = placed.tile([P, S], U8, name="x2s_g", align_bytes=64, offset=0)
        nc.vector.tensor_copy(x2s_g[:], xs_win[:].indirect(two_t[:]))
        x2_sc = rows[:, 2 * S : 3 * S]
        move_rows(nc.sync, x2_sc, x2s_g[:])
        ws_raw = new("ws_raw", [P, S], U8, "after_dw_win")
        for i, scales in enumerate((w1_scales, w2_scales)):
            for j in range(4):
                nc.sync.dma_start(ws_raw[4 * i + j : P : 8, :].bitcast(I32), spread(scales[0, j:16:4, :], 4))

        w_d = new("w_d", [P, 2, S], U32)
        for i in range(2):
            deal(w_d[:, i, :], w_raw[:, i, :])

        minus_half_pa = [new(f"minus_half_pa{t}", [P, W], F32) for t in range(PACK)]
        old_less = [new(f"old_less{t}", [P, W], F32) for t in range(PACK)]
        ra = [new(f"ra{t}", [P, W], F32) for t in range(PACK)]
        h_out(0)
        for k in range(PACK + 1):
            if k + 1 < PACK:
                h_out(k + 1)
            if k < PACK:
                nc.scalar.activation(minus_half_pa[k][:], h[k][:].indirect(n2_t[:]), ACT.Copy, scale=-0.5)
                nc.vector.tensor_tensor(old_less[k][:], h[k][:].indirect(n1_t[:]), minus_half_pa[k][:], ALU.add)
            if k >= 1:
                nc.vector.scalar_tensor_tensor(ra[k - 1][:], minus_half_pa[k - 1][:], -1.0, old_less[k - 1][:], ALU.mult, ALU.min)

        for t in range(2):
            nc.scalar.activation(h[t][:].indirect(n1_t[:]), ra[t][:], ACT.Copy)
        nc.vector.tensor_copy(h[2][:].indirect(entries(n1_t, 0, VECTOR_ENTRIES)), ra[2][:, 0:VECTOR_ENTRIES])
        nc.vector.tensor_copy(h[3][:].indirect(n1_t[:]), ra[3][:])
        nc.scalar.activation(h[2][:].indirect(entries(n1_t, VECTOR_ENTRIES, W)), ra[2][:, VECTOR_ENTRIES:W], ACT.Copy)
        ws_d = new("ws_d", [P, S], U8)
        deal(ws_d[:], ws_raw[:])

        z_tiles = new("z_tiles", [P, PACK, S], BF16, "after_dw_win")
        h2p = {}
        for t in range(PACK):
            for i in range(2):
                c = slice(P * t, P * (t + 1))
                cols = slice(HALF * i, HALF * (i + 1))
                h2p[t, i] = ps.tile([P, HALF], F32, name=f"h2p{t}_{i}", tag=f"bank{PACK * i + t}")
                nc.tensor.matmul_mx(h2p[t, i][:], lhsT=w_d[:, 1, c].bitcast(FP8X4), lhsT_scale=ws_d[4:P, c],
                                    rhs=x2w_g[:, cols].bitcast(FP8X4), rhs_scale=x2_sc[:, cols], start=True, stop=False)
        for t in (0, 1, 3):
            nc.vector.tensor_scalar(z_tiles[:, t, :], h[t][:], gn_t[:, t : t + 1], None, ALU.mult)
        for cols in (slice(0, HALF), slice(HALF, SCALAR_FROM)):
            nc.vector.tensor_scalar(z_tiles[:, 2, cols], h[2][:, cols], gn_t[:, 2:3], None, ALU.mult)
        nc.scalar.activation(z_tiles[:, 2, SCALAR_FROM:S], h[2][:, SCALAR_FROM:S], ACT.Copy, scale=gn_t[:, 2:3])

        def interleave_on_vector(dst, src):
            nc.vector.tensor_copy(dst.rearrange("p (c i) t -> p c t i", i=4), src.rearrange("p t (c i) -> p c t i", i=4))

        def interleave_on_scalar(dst, src):
            nc.scalar.copy(dst, src.rearrange("p t c -> p c t"))

        z_il = [new(f"z_il{i}", [P, HALF, PACK], BF16) for i in range(2)]
        z_w = [new(f"z_w{i}", [P, HALF], U32) for i in range(2)]
        z_s = [new(f"z_s{i}", [P, HALF], U8) for i in range(2)]
        interleave_on_vector(z_il[0][:], z_tiles[:, :, 0:HALF])
        interleave_on_scalar(z_il[1][:, SCALAR_FROM - HALF : HALF, :], z_tiles[:, :, SCALAR_FROM:S])
        interleave_on_vector(z_il[1][:, 0 : SCALAR_FROM - HALF, :], z_tiles[:, :, HALF:SCALAR_FROM])
        for i in range(2):
            nc.vector.quantize_mx(z_w[i][:].bitcast(FP8X4), z_s[i][:], z_il[i][:].rearrange("p c t -> p (c t)"))
        for t, i in [(0, 0), (1, 0), (0, 1), (1, 1)] + [(t, i) for t in (2, 3) for i in range(2)]:
            c = slice(P * t, P * (t + 1))
            nc.tensor.matmul_mx(h2p[t, i][:], lhsT=w_d[:, 0, c].bitcast(FP8X4), lhsT_scale=ws_d[:, c],
                                rhs=z_w[i][:].bitcast(FP8X4), rhs_scale=z_s[i][:], start=False, stop=True)

        h2 = [new(f"h2_{t}", [P, S], F32) for t in range(PACK)]
        size = [new(f"size{t}", [P, S], F32) for t in range(PACK)]
        out_rows = out_0.rearrange("(p t) c -> p t c", t=PACK)
        o_w = new("o_w", [P, S], U32)
        o_s = new("o_s", [P, S], U8)
        pieces = [(i, t) for i in range(2) for t in range(PACK)]
        y = [new(f"y{i}", [P, PACK, HALF], F32) for i in range(2)]
        sums, roots = {}, {}

        def add_sizes(i, t):
            c0 = HALF * i
            fetched = new(f"fetched{i}_{t}", [P, HALF], F32)
            looked_up = size[t][:].indirect(entries(n4_t, c0, c0 + HALF))
            if i == 0:
                nc.vector.tensor_copy(fetched[:], looked_up)
            else:
                nc.scalar.activation(fetched[:], looked_up, ACT.Copy)
            sums[i, t] = ps.tile([P, HALF], F32, name=f"sum{i}_{t}", tag=f"bank{t}")
            for b in range(0, HALF, P):
                block = sums[i, t][:, b : b + P]
                nc.tensor.matmul(block, lhsT=size[t][:, c0 + b : c0 + b + P], rhs=ident[:], is_transpose=True, start=True, stop=False)
                nc.tensor.matmul(block, lhsT=fetched[:, b : b + P], rhs=ident[:], is_transpose=True, start=False, stop=True)

        def inverse_root(i, t):
            root_t = new(f"root_t{i}_{t}", [P, HALF], F32)
            nc.scalar.activation(root_t[:], sums[i, t][:], ACT.Abs_reciprocal_sqrt, bias=half[:])
            roots[i, t] = ps.tile([P, HALF], F32, name=f"root{i}_{t}", tag=f"bank{PACK + t}")
            for b in range(0, HALF, P):
                nc.tensor.transpose(roots[i, t][:, b : b + P], root_t[:, b : b + P], ident[:])

        def divide(i, t):
            c0 = HALF * i
            inverse = new(f"inverse{i}_{t}", [P, HALF], F32)
            nc.scalar.activation(inverse[:], roots[i, t][:], ACT.Square)
            width = P if (i, t) == pieces[-1] else HALF
            for b in range(0, HALF, width):
                looked_up = h2[t][:].indirect(entries(n3_t, c0 + b, c0 + b + width))
                nc.vector.tensor_tensor(y[i][:, t, b : b + width], looked_up, inverse[:, b : b + width], ALU.mult)
            nc.sync.dma_start(out_rows[:, t, c0 : c0 + HALF], y[i][:, t, :])

        def leave_banks(t):
            for i in range(2):
                nc.scalar.activation(size[t][:, HALF * i : HALF * (i + 1)], h2p[t, i][:], ACT.Abs)
            for i in (1, 0):
                nc.vector.tensor_copy(h2[t][:, HALF * i : HALF * (i + 1)], h2p[t, i][:])

        leave_banks(0)
        for step in range(len(pieces) + 2):
            if step + 1 < PACK:
                leave_banks(step + 1)
            if step < len(pieces):
                add_sizes(*pieces[step])
            if 1 <= step <= len(pieces):
                inverse_root(*pieces[step - 1])
            if step >= 2:
                divide(*pieces[step - 2])

        y_il = [new("y_il0", [P, HALF, PACK], BF16, "root_t1_3")]
        interleave_on_scalar(y_il[0][:], y[0][:])
        for b in (0, P):
            y_il.append(new(f"y_il1_{b}", [P, P, PACK], BF16))
            interleave_on_vector(y_il[-1][:], y[1][:, :, b : b + P])
        for part, cols in zip(y_il, (slice(0, HALF), slice(HALF, HALF + P), slice(HALF + P, S))):
            nc.vector.quantize_mx(o_w[:, cols].bitcast(FP8X4), o_s[:, cols], part[:].rearrange("p c t -> p (c t)"))
            nc.sync.dma_start(words_of(out_1)[:, cols], o_w[:, cols].bitcast(I32))
        for q in range(4):
            eng = nc.sync if q % 2 == 0 else nc.scalar
            eng.dma_start(out_2[0, 4 * q : 4 * q + 4, :].bitcast(I32), o_s[32 * q : 32 * q + 4, :].bitcast(I32))
